import numpy as np
import ml_dtypes


def mxq(x, axis, fmt="e4m3"):
    dtype, down = {"e4m3": (ml_dtypes.float8_e4m3fn, 7), "e5m2": (ml_dtypes.float8_e5m2, 14)}[fmt]
    v = np.moveaxis(np.asarray(x, np.float32).astype(ml_dtypes.bfloat16).astype(np.float64), axis, -1)
    blocks = v.reshape(v.shape[:-1] + (-1, 32))
    amax = np.abs(blocks).max(-1, keepdims=True)
    byte = np.maximum(np.where(amax > 0, np.frexp(amax)[1] - 1 + 127, 0) - down, 1)
    scale = np.exp2(byte - 127.0)
    codes = (blocks / scale).astype(np.float32).astype(dtype).astype(np.float64)
    return np.moveaxis((codes * scale).reshape(v.shape), -1, axis)


WIDE = False


def mx_kscale(k, group=512):
    if not WIDE:
        return np.ones(k)
    levels = np.array([10, -10, 5, -5, 0])
    if group != 512:
        return np.exp2(np.random.permutation(np.resize(levels, k // group))).repeat(group)
    if k % 512:
        return np.exp2(np.random.permutation(np.resize(levels, k // 32))).repeat(32)
    a = np.empty((k // 512, 16))
    for p in range(k // 512):
        a[p, :8] = np.random.permutation(np.resize(levels, 8))
        for g in range(8):
            far = levels[np.abs(levels - a[p, g]) >= 10]
            a[p, g + 8] = far[np.random.randint(len(far))]
    return np.exp2(a.ravel()).repeat(32)


def f64(x):
    return np.asarray(x).astype(np.float64)


def striped(idx):
    return np.tile(np.asarray(idx).reshape(-1, 16).T, (8, 1)).astype(np.uint16)


def unstriped(offs):
    return offs[:16].T.reshape(-1).astype(np.int64)


H, KV, D, NQ, N = 2, 2, 256, 512, 1024


def setup_inputs():
    n = np.random.standard_normal
    s = mx_kscale(D, 0)[:, None]
    u = mx_kscale(N)
    t = np.random.uniform(0.5, 2.0, N) * u
    v = n((KV, N, 128))
    v[:, :, 127] = 1.0
    return {
        "qT": (n((H, D, NQ)) * s * (0.70 / np.sqrt(D))).astype(np.float32),
        "kT": (n((KV, D, N)) / s).astype(np.float32),
        "t": t.reshape(N, 1).astype(np.float32),
        "v": (v / t[:, None]).astype(np.float32),
        "mask": (np.arange(N)[:, None] <= np.sort(np.random.randint(N // 4, N, NQ))[None, :]).astype(np.float32),
        "sink": (N * np.random.uniform(0.1, 1.0, (H, NQ, 1))).astype(np.float32),
    }


def reference(qT, kT, t, v, mask, sink):
    a = mxq(f64(kT), 1, "e4m3").transpose(0, 2, 1) @ mxq(f64(qT), 1, "e4m3")
    p = np.exp(a)
    p = p * f64(mask)
    w = p * f64(t)
    y = mxq(w, 1, "e4m3").transpose(0, 2, 1) @ mxq(f64(v), 1, "e4m3")
    y = y / (y[:, :, 127:128] + f64(sink))
    return y

@@ -1,0 +1,246 @@
+from contextlib import ExitStack
+
+import concourse.mybir as mybir
+
+H, D, NQ, N, E = 2, 256, 512, 1024, 128
+FLOPS = 2 * H * N * NQ * (D + E)
+
+F32 = mybir.dt.float32
+BF16 = mybir.dt.bfloat16
+U32 = mybir.dt.uint32
+U8 = mybir.dt.uint8
+X4 = mybir.dt.float8_e4m3fn_x4
+ACT = mybir.ActivationFunctionType
+ALU = mybir.AluOpType
+P = 128
+
+QCH = [[0,1],[2,3]]
+MCH = [[[0,1],[2,3]],[[0,1],[2,3]]]
+ORDER = """
+wa dk0 dk1 dq0 dq1 dt dm00 dm01 dk2 dm10 dv0 dm11 dv1 ds
+ik003 qk003 ik103 qk103 iq00 iq11:S qq00 qq11
+sc000 sc001 sc010 sc011 ex000 ex001 ex010 ex011
+iq23 mt0003 qq23
+sc020 sc021 sc030 sc031
+ww0001 ex020 ex021 mt0103:S ww0101 qw0001 ex030 ex031
+ik201 qw0101 ik223:S qk201 ww0023 qk223 
+sc100 sc101 sc110 sc111 mt1001:S ex100 ex101
+mt1023 ww0123 qw0023 ex110 ex111 sc120 sc121 sc130 sc131
+iv00:S iv01:S
+ww1001 qw0123 qv0 ex120 ex121 ww1101 qw1001 mt1103 iv10:S iv11:S qw1101
+yy00 yy10 ex130 ex131
+ww1022 qv1 yy01 yy11 de00:S de10:S ww1122 re000 qw1022 re100 oo00:S de01:S de11:S oo10:S yy20
+ww1033 re011 qw1122 re111 oo01:S oo11:S yy21 de20:S ww1133 re200 qw1033 yy30 de21:S oo20:S qw1133 yy31 re211 oo21:S de30 re300 oo30:S de31 re311 oo31
+"""
+
+
+def tile_rows_sink_mask_kernel(tc, qT, kT, t, v, mask, sink, out):
+    nc = tc.nc
+    with ExitStack() as ctx:
+        sb = ctx.enter_context(tc.tile_pool(name="sb", bufs=1))
+        ps = ctx.enter_context(tc.psum_pool(name="ps", bufs=1))
+
+        def mk(name, shape, dt):
+            return sb.tile(shape, dt, name=name, align_bytes=64)
+
+        q_hbm = qT.rearrange("h (p j) q -> (h p) j q", j=4)
+        k_hbm = kT.rearrange("h (p j) n -> (h p) j n", j=4)
+        m_hbm = mask.rearrange("(c p j) q -> c p j q", p=P, j=4)
+
+        q_raw = [mk("q_raw%d" % i, [P, 4, P * len(g)], F32) for i, g in enumerate(QCH)]
+        q_at = {qt: (i, n) for i, g in enumerate(QCH) for n, qt in enumerate(g)}
+        q_bf = mk("q_bf", [P, NQ, 4], BF16)
+        q_codes = mk("q_codes", [P, NQ], U32)
+        q_scales = mk("q_scales", [P, NQ], U8)
+        k0_raw = [mk("k0_raw%d" % i, [P, 4, 256], F32) for i in range(2)]
+        k0_bf = [mk("k0_bf%d" % i, [P, 4, 64, 4], BF16) for i in range(2)]
+        k1_raw = mk("k1_raw", [P, 4, 512], F32)
+        k1_bf = mk("k1_bf", [P, 4, P, 4], BF16)
+        k_codes = [mk("k_codes%d" % c, [P, 4, P], U32) for c in range(2)]
+        k_scales = [mk("k_scales%d" % c, [P, 4, P], U8) for c in range(2)]
+        m_raw = [[mk("m_raw%d_%d" % (c, i), [P, 4, P * len(g)], F32) for i, g in enumerate(MCH[c])] for c in range(2)]
+        mt = [[mk("mt%d_%d" % (c, i), [P, 4, P * len(g)], F32) for i, g in enumerate(MCH[c])] for c in range(2)]
+        m_at = [{qt: (i, n) for i, g in enumerate(MCH[c]) for n, qt in enumerate(g)} for c in range(2)]
+        t_sb = mk("t_sb", [P, 2, 8], F32)
+        sink_sb = mk("sink_sb", [P, H, 4, 8], F32)
+        v_raw = [mk("v_raw%d" % h, [P, 2, 4, E], F32) for h in range(H)]
+        v_bf = [mk("v_bf%d" % h, [P, 2, E, 4], BF16) for h in range(H)]
+        v_codes = [mk("v_codes%d" % h, [P, 2, E], U32) for h in range(H)]
+        v_scales = [mk("v_scales%d" % h, [P, 2, E], U8) for h in range(H)]
+        pe = [[mk("pe%d_%d" % (c, h), [P, 4, 512], F32) for h in range(H)] for c in range(2)]
+        w_bf = [[mk("w_bf%d_%d" % (c, h), [P, NQ, 4], BF16) for h in range(H)] for c in range(2)]
+        w_codes = [[mk("w_codes%d_%d" % (c, h), [P, NQ], U32) for h in range(H)] for c in range(2)]
+        w_scales = [[mk("w_scales%d_%d" % (c, h), [P, NQ], U8) for h in range(H)] for c in range(2)]
+        den = mk("den", [P, 4, H], F32)
+        rec = mk("rec", [P, 4, H], F32)
+        res = [[mk("res%d_%d" % (qt, h), [P, E], F32) for h in range(H)] for qt in range(4)]
+        warm = mk("warm", [P, 8], F32)
+        s_bank = [[ps.tile([P, 4, P], F32, name="s_bank%d_%d" % (h, b)) for b in range(2)] for h in range(H)]
+        y_bank = [ps.tile([P, 512], F32, name="y_bank%d" % b) for b in range(4)]
+
+        def copy(eng, o, i):
+            if eng == "V":
+                nc.vector.tensor_copy(out=o, in_=i)
+            else:
+                nc.scalar.copy(out=o, in_=i)
+
+        def quant(codes, scales, src):
+            nc.vector.quantize_mx(out=codes.bitcast(X4), scales=scales, in_=src)
+
+        def run(op):
+            name, eng = op.split(":") if len(op.split(":")) == 2 else (op, "V")
+            kind, a = name[:2], [int(ch) for ch in name[2:]]
+            if kind == "wa":
+                nc.gpsimd.memset(warm[:, 0:1], 0.0)
+                nc.scalar.activation(out=warm[:, 4:5], in_=warm[:, 0:1], func=ACT.Exp)
+            elif kind == "dq":
+                g = QCH[a[0]]
+                nc.sync.dma_start(out=q_raw[a[0]][:], in_=q_hbm[:, :, P * g[0] : P * (g[-1] + 1)])
+            elif kind == "dk":
+                if a[0] < 2:
+                    nc.sync.dma_start(out=k0_raw[a[0]][:], in_=k_hbm[:, :, 256 * a[0] : 256 * (a[0] + 1)])
+                else:
+                    nc.sync.dma_start(out=k1_raw[:], in_=k_hbm[:, :, 512:1024])
+            elif kind == "dm":
+                g = MCH[a[0]][a[1]]
+                nc.sync.dma_start(out=m_raw[a[0]][a[1]][:], in_=m_hbm[a[0]][:, :, P * g[0] : P * (g[-1] + 1)])
+            elif kind == "dv":
+                nc.sync.dma_start(out=v_raw[a[0]][:], in_=v[a[0]].rearrange("(c p j) e -> p c j e", p=P, j=4))
+            elif kind == "dt":
+                nc.sync.dma_start(out=t_sb[:, :, 0:4], in_=t.rearrange("(c p j) o -> p c (j o)", p=P, j=4))
+            elif kind == "ds":
+                with nc.allow_non_contiguous_dma(reason="one sink a query row"):
+                    nc.sync.dma_start(
+                        out=sink_sb[:].rearrange("p h a x -> p (h a) x")[:, :, 0:1],
+                        in_=sink.rearrange("h (a p) o -> p (h a) o", p=P),
+                    )
+            elif kind == "iq":
+                i, n = q_at[a[0]]
+                cnt = a[-1] - a[0] + 1
+                copy(
+                    eng,
+                    q_bf[:, P * a[0] : P * (a[-1] + 1), :].rearrange("p (a i) j -> p a j i", i=2),
+                    q_raw[i][:, :, P * n : P * (n + cnt)].rearrange("p j (a i) -> p a j i", i=2),
+                )
+            elif kind == "qq":
+                cols = slice(P * a[0], P * (a[-1] + 1))
+                quant(q_codes[:, cols], q_scales[:, cols], q_bf[:, cols, :].rearrange("p q j -> p (q j)"))
+            elif kind == "ik":
+                raw, bf = (k0_raw[a[0]], k0_bf[a[0]]) if a[0] < 2 else (k1_raw, k1_bf)
+                rs = slice(a[1], a[2] + 1)
+                copy(
+                    eng,
+                    bf[:, rs].rearrange("p r s j -> p s r j"),
+                    raw[:].rearrange("p j (s r) -> p s r j", r=4)[:, :, rs, :],
+                )
+            elif kind == "qk":
+                if a[0] < 2:
+                    cols = slice(64 * a[0], 64 * (a[0] + 1))
+                    for r in range(a[1], a[2] + 1):
+                        quant(k_codes[0][:, r, cols], k_scales[0][:, r, cols], k0_bf[a[0]][:, r].rearrange("p s j -> p (s j)"))
+                else:
+                    rs = slice(a[1], a[2] + 1)
+                    quant(
+                        k_codes[1][:, rs].rearrange("p r s -> p (r s)"),
+                        k_scales[1][:, rs].rearrange("p r s -> p (r s)"),
+                        k1_bf[:, rs].rearrange("p r s j -> p (r s j)"),
+                    )
+            elif kind == "iv":
+                h, c = a
+                copy(
+                    eng,
+                    v_bf[h][:, c].rearrange("p (a i) j -> p a j i", i=2),
+                    v_raw[h][:, c].rearrange("p j (a i) -> p a j i", i=2),
+                )
+            elif kind == "qv":
+                h = a[0]
+                quant(
+                    v_codes[h][:].rearrange("p c e -> p (c e)"),
+                    v_scales[h][:].rearrange("p c e -> p (c e)"),
+                    v_bf[h][:].rearrange("p c e j -> p (c e j)"),
+                )
+            elif kind == "mt":
+                c, i = a[0], a[1]
+                for j in range(a[2], a[3] + 1):
+                    if eng == "V":
+                        nc.vector.tensor_scalar(
+                            out=mt[c][i][:, j], in0=m_raw[c][i][:, j], scalar1=t_sb[:, c, j : j + 1], scalar2=None, op0=ALU.mult
+                        )
+                    else:
+                        nc.scalar.activation(out=mt[c][i][:, j], in_=m_raw[c][i][:, j], func=ACT.Copy, scale=t_sb[:, c, j : j + 1])
+            elif kind == "sc":
+                c, qt, h = a
+                rows = slice(64 * h, 64 * (h + 1))
+                cols = slice(P * qt, P * (qt + 1))
+                for r in range(4):
+                    nc.tensor.matmul_mx(
+                        out=s_bank[h][qt % 2][:, r, :],
+                        lhsT=k_codes[c][rows, r, :].bitcast(X4),
+                        lhsT_scale=k_scales[c][rows, r, :],
+                        rhs=q_codes[rows, cols].bitcast(X4),
+                        rhs_scale=q_scales[rows, cols],
+                        start=True,
+                        stop=True,
+                    )
+            elif kind == "ex":
+                c, qt, h = a
+                nc.scalar.activation(
+                    out=pe[c][h][:, qt].rearrange("p (a r i) -> p a r i", r=4, i=2),
+                    in_=s_bank[h][qt % 2][:].rearrange("p r (a i) -> p a r i", i=2),
+                    func=ACT.Exp,
+                )
+            elif kind == "ww":
+                c, h, q0, q1 = a
+                i, n = m_at[c][q0]
+                cnt = q1 - q0 + 1
+                nc.vector.tensor_tensor(
+                    out=w_bf[c][h][:, P * q0 : P * (q1 + 1), :].rearrange("p (a i) r -> p a r i", i=2),
+                    in0=pe[c][h][:, q0 : q1 + 1].rearrange("p b (a r i) -> p (b a) r i", r=4, i=2),
+                    in1=mt[c][i][:, :, P * n : P * (n + cnt)].rearrange("p r (a i) -> p a r i", i=2),
+                    op=ALU.mult,
+                )
+            elif kind == "qw":
+                c, h, q0, q1 = a
+                cols = slice(P * q0, P * (q1 + 1))
+                quant(w_codes[c][h][:, cols], w_scales[c][h][:, cols], w_bf[c][h][:, cols, :].rearrange("p q j -> p (q j)"))
+            elif kind == "yy":
+                qt, h = a
+                cols = slice(P * qt, P * (qt + 1))
+                for c in range(2):
+                    nc.tensor.matmul_mx(
+                        out=y_bank[(2 * qt + h) % 4][:, 0:E],
+                        lhsT=w_codes[c][h][:, cols].bitcast(X4),
+                        lhsT_scale=w_scales[c][h][:, cols],
+                        rhs=v_codes[h][:, c, :].bitcast(X4),
+                        rhs_scale=v_scales[h][:, c, :],
+                        start=(c == 0),
+                        stop=(c == 1),
+                    )
+            elif kind == "de":
+                qt, h = a
+                y = y_bank[(2 * qt + h) % 4]
+                if eng == "V":
+                    nc.vector.tensor_scalar(
+                        out=den[:, qt, h : h + 1], in0=y[:, E - 1 : E], scalar1=sink_sb[:, h, qt, 0:1], scalar2=None, op0=ALU.add
+                    )
+                else:
+                    nc.scalar.activation(out=den[:, qt, h : h + 1], in_=y[:, E - 1 : E], func=ACT.Identity, bias=sink_sb[:, h, qt, 0:1])
+            elif kind == "re":
+                qt, h0, h1 = a
+                nc.vector.reciprocal(out=rec[:, qt, h0 : h1 + 1], in_=den[:, qt, h0 : h1 + 1])
+            elif kind == "oo":
+                qt, h = a
+                y = y_bank[(2 * qt + h) % 4]
+                if eng == "V":
+                    nc.vector.tensor_scalar(
+                        out=res[qt][h][:], in0=y[:, 0:E], scalar1=rec[:, qt, h : h + 1], scalar2=None, op0=ALU.mult
+                    )
+                else:
+                    nc.scalar.activation(out=res[qt][h][:], in_=y[:, 0:E], func=ACT.Copy, scale=rec[:, qt, h : h + 1])
+                nc.sync.dma_start(out=out[h, P * qt : P * (qt + 1), :], in_=res[qt][h][:])
+            else:
+                raise ValueError(op)
+
+        with tc.manual_schedule():
+            for op in ORDER.split():
+                run(op)

@@ -2,245 +2,348 @@ from contextlib import ExitStack
 
 import concourse.mybir as mybir
 
-H, D, NQ, N, E = 2, 256, 512, 1024, 128
-FLOPS = 2 * H * N * NQ * (D + E)
+HEADS, FEATURES, QUERIES, TOKENS, VALUES = 2, 256, 512, 1024, 128
+FLOPS = 2 * HEADS * TOKENS * QUERIES * (FEATURES + VALUES)
 
 F32 = mybir.dt.float32
 BF16 = mybir.dt.bfloat16
 U32 = mybir.dt.uint32
 U8 = mybir.dt.uint8
-X4 = mybir.dt.float8_e4m3fn_x4
+FP8X4 = mybir.dt.float8_e4m3fn_x4
 ACT = mybir.ActivationFunctionType
 ALU = mybir.AluOpType
-P = 128
 
-QCH = [[0,1],[2,3]]
-MCH = [[[0,1],[2,3]],[[0,1],[2,3]]]
-ORDER = """
-wa dk0 dk1 dq0 dq1 dt dm00 dm01 dk2 dm10 dv0 dm11 dv1 ds
-ik003 qk003 ik103 qk103 iq00 iq11:S qq00 qq11
-sc000 sc001 sc010 sc011 ex000 ex001 ex010 ex011
-iq23 mt0003 qq23
-sc020 sc021 sc030 sc031
-ww0001 ex020 ex021 mt0103:S ww0101 qw0001 ex030 ex031
-ik201 qw0101 ik223:S qk201 ww0023 qk223 
-sc100 sc101 sc110 sc111 mt1001:S ex100 ex101
-mt1023 ww0123 qw0023 ex110 ex111 sc120 sc121 sc130 sc131
-iv00:S iv01:S
-ww1001 qw0123 qv0 ex120 ex121 ww1101 qw1001 mt1103 iv10:S iv11:S qw1101
-yy00 yy10 ex130 ex131
-ww1022 qv1 yy01 yy11 de00:S de10:S ww1122 re000 qw1022 re100 oo00:S de01:S de11:S oo10:S yy20
-ww1033 re011 qw1122 re111 oo01:S oo11:S yy21 de20:S ww1133 re200 qw1033 yy30 de21:S oo20:S qw1133 yy31 re211 oo21:S de30 re300 oo30:S de31 re311 oo31
-"""
+P = 128
+PACK = 4
+HEAD_ROWS = FEATURES // PACK
+PASS = P * PACK
+PASSES = TOKENS // PASS
+TILES = QUERIES // P
+HALF = QUERIES // 2
+BLOCK = 32
+RUN = 2
+
+KEY_LOADS = ((0, PASS // 2), (PASS // 2, PASS), (PASS, 2 * PASS))
+QUERY_LOADS = ((0,), (1, 2, 3))
+LOW, HIGH, ALL_PLACES = range(0, 2), range(2, 4), range(0, 4)
+BOTH_HEADS = (0, 1)
+LAST_TILE = TILES - 1
 
 
 def tile_rows_sink_mask_kernel(tc, qT, kT, t, v, mask, sink, out):
     nc = tc.nc
+    vector, scalar = "vector", "scalar"
+
     with ExitStack() as ctx:
-        sb = ctx.enter_context(tc.tile_pool(name="sb", bufs=1))
-        ps = ctx.enter_context(tc.psum_pool(name="ps", bufs=1))
+        sbuf = ctx.enter_context(tc.tile_pool(name="sbuf", bufs=1))
+        psum = ctx.enter_context(tc.psum_pool(name="psum", bufs=1))
 
-        def mk(name, shape, dt):
-            return sb.tile(shape, dt, name=name, align_bytes=64)
+        def tile(name, shape, dtype):
+            return sbuf.tile(shape, dtype, name=name, align_bytes=64)
 
-        q_hbm = qT.rearrange("h (p j) q -> (h p) j q", j=4)
-        k_hbm = kT.rearrange("h (p j) n -> (h p) j n", j=4)
-        m_hbm = mask.rearrange("(c p j) q -> c p j q", p=P, j=4)
+        q_raw = [tile("q_raw%d" % n, [P, PACK, P * len(tiles)], F32) for n, tiles in enumerate(QUERY_LOADS)]
+        q_bf = tile("q_bf", [P, QUERIES, PACK], BF16)
+        q_codes = tile("q_codes", [P, QUERIES], U32)
+        q_scales = tile("q_scales", [P, QUERIES], U8)
+        k_raw = [tile("k_raw%d" % n, [P, PACK, hi - lo], F32) for n, (lo, hi) in enumerate(KEY_LOADS)]
+        k_bf = [tile("k_bf%d" % n, [P, PACK, (hi - lo) // PACK, PACK], BF16) for n, (lo, hi) in enumerate(KEY_LOADS)]
+        k_codes = [tile("k_codes%d" % c, [P, PACK, P], U32) for c in range(PASSES)]
+        k_scales = [tile("k_scales%d" % c, [P, PACK, P], U8) for c in range(PASSES)]
+        mask_raw = [[tile("mask_raw%d_%d" % (c, n), [P, PACK, HALF], F32) for n in range(2)] for c in range(PASSES)]
+        mask_t = [[tile("mask_t%d_%d" % (c, n), [P, PACK, HALF], F32) for n in range(2)] for c in range(PASSES)]
+        t_cols = tile("t_cols", [P, PASSES, 2 * PACK], F32)
+        sink_rows = tile("sink_rows", [P, BLOCK], F32)
+        sink_cols = tile("sink_cols", [P, BLOCK], F32)
+        v_raw = [tile("v_raw%d" % h, [P, PASSES, PACK, VALUES], F32) for h in BOTH_HEADS]
+        v_bf = [tile("v_bf%d" % h, [P, PASSES, VALUES, PACK], BF16) for h in BOTH_HEADS]
+        v_codes = [tile("v_codes%d" % h, [P, PASSES, VALUES], U32) for h in BOTH_HEADS]
+        v_scales = [tile("v_scales%d" % h, [P, PASSES, VALUES], U8) for h in BOTH_HEADS]
+        exps = [[tile("exps%d_%d" % (c, h), [P, TILES, PACK * P], F32) for h in BOTH_HEADS] for c in range(PASSES)]
+        w_bf = [[tile("w_bf%d_%d" % (c, h), [P, QUERIES, PACK], BF16) for h in BOTH_HEADS] for c in range(PASSES)]
+        w_codes = [[tile("w_codes%d_%d" % (c, h), [P, QUERIES], U32) for h in BOTH_HEADS] for c in range(PASSES)]
+        w_scales = [[tile("w_scales%d_%d" % (c, h), [P, QUERIES], U8) for h in BOTH_HEADS] for c in range(PASSES)]
+        denom = tile("denom", [P, TILES, HEADS], F32)
+        inverse = tile("inverse", [P, TILES, HEADS], F32)
+        result = [tile("result%d" % qt, [P, HEADS, VALUES], F32) for qt in range(TILES)]
 
-        q_raw = [mk("q_raw%d" % i, [P, 4, P * len(g)], F32) for i, g in enumerate(QCH)]
-        q_at = {qt: (i, n) for i, g in enumerate(QCH) for n, qt in enumerate(g)}
-        q_bf = mk("q_bf", [P, NQ, 4], BF16)
-        q_codes = mk("q_codes", [P, NQ], U32)
-        q_scales = mk("q_scales", [P, NQ], U8)
-        k0_raw = [mk("k0_raw%d" % i, [P, 4, 256], F32) for i in range(2)]
-        k0_bf = [mk("k0_bf%d" % i, [P, 4, 64, 4], BF16) for i in range(2)]
-        k1_raw = mk("k1_raw", [P, 4, 512], F32)
-        k1_bf = mk("k1_bf", [P, 4, P, 4], BF16)
-        k_codes = [mk("k_codes%d" % c, [P, 4, P], U32) for c in range(2)]
-        k_scales = [mk("k_scales%d" % c, [P, 4, P], U8) for c in range(2)]
-        m_raw = [[mk("m_raw%d_%d" % (c, i), [P, 4, P * len(g)], F32) for i, g in enumerate(MCH[c])] for c in range(2)]
-        mt = [[mk("mt%d_%d" % (c, i), [P, 4, P * len(g)], F32) for i, g in enumerate(MCH[c])] for c in range(2)]
-        m_at = [{qt: (i, n) for i, g in enumerate(MCH[c]) for n, qt in enumerate(g)} for c in range(2)]
-        t_sb = mk("t_sb", [P, 2, 8], F32)
-        sink_sb = mk("sink_sb", [P, H, 4, 8], F32)
-        v_raw = [mk("v_raw%d" % h, [P, 2, 4, E], F32) for h in range(H)]
-        v_bf = [mk("v_bf%d" % h, [P, 2, E, 4], BF16) for h in range(H)]
-        v_codes = [mk("v_codes%d" % h, [P, 2, E], U32) for h in range(H)]
-        v_scales = [mk("v_scales%d" % h, [P, 2, E], U8) for h in range(H)]
-        pe = [[mk("pe%d_%d" % (c, h), [P, 4, 512], F32) for h in range(H)] for c in range(2)]
-        w_bf = [[mk("w_bf%d_%d" % (c, h), [P, NQ, 4], BF16) for h in range(H)] for c in range(2)]
-        w_codes = [[mk("w_codes%d_%d" % (c, h), [P, NQ], U32) for h in range(H)] for c in range(2)]
-        w_scales = [[mk("w_scales%d_%d" % (c, h), [P, NQ], U8) for h in range(H)] for c in range(2)]
-        den = mk("den", [P, 4, H], F32)
-        rec = mk("rec", [P, 4, H], F32)
-        res = [[mk("res%d_%d" % (qt, h), [P, E], F32) for h in range(H)] for qt in range(4)]
-        warm = mk("warm", [P, 8], F32)
-        s_bank = [[ps.tile([P, 4, P], F32, name="s_bank%d_%d" % (h, b)) for b in range(2)] for h in range(H)]
-        y_bank = [ps.tile([P, 512], F32, name="y_bank%d" % b) for b in range(4)]
+        score_bank = [[psum.tile([P, PACK, P], F32, name="score_bank%d_%d" % (h, b)) for b in range(2)] for h in BOTH_HEADS]
+        y_bank = [psum.tile([P, PACK * P], F32, name="y_bank%d" % b) for b in range(TILES)]
 
-        def copy(eng, o, i):
-            if eng == "V":
-                nc.vector.tensor_copy(out=o, in_=i)
+        def y_of(qt, h):
+            if (qt, h) == (LAST_TILE, 1):
+                return y_bank[0][:, 0:VALUES]
+            return y_bank[qt][:, VALUES * h : VALUES * (h + 1)]
+
+        def rows_of(first, last):
+            return slice(P * first, P * (last + 1))
+
+        def cast(engine, dst, src):
+            if engine == vector:
+                nc.vector.tensor_copy(out=dst, in_=src)
             else:
-                nc.scalar.copy(out=o, in_=i)
+                nc.scalar.copy(out=dst, in_=src)
 
-        def quant(codes, scales, src):
-            nc.vector.quantize_mx(out=codes.bitcast(X4), scales=scales, in_=src)
+        def times_column(engine, dst, src, column):
+            if engine == vector:
+                nc.vector.tensor_scalar(out=dst, in0=src, scalar1=column, scalar2=None, op0=ALU.mult)
+            else:
+                nc.scalar.activation(out=dst, in_=src, func=ACT.Copy, scale=column)
 
-        def run(op):
-            name, eng = op.split(":") if len(op.split(":")) == 2 else (op, "V")
-            kind, a = name[:2], [int(ch) for ch in name[2:]]
-            if kind == "wa":
-                nc.gpsimd.memset(warm[:, 0:1], 0.0)
-                nc.scalar.activation(out=warm[:, 4:5], in_=warm[:, 0:1], func=ACT.Exp)
-            elif kind == "dq":
-                g = QCH[a[0]]
-                nc.sync.dma_start(out=q_raw[a[0]][:], in_=q_hbm[:, :, P * g[0] : P * (g[-1] + 1)])
-            elif kind == "dk":
-                if a[0] < 2:
-                    nc.sync.dma_start(out=k0_raw[a[0]][:], in_=k_hbm[:, :, 256 * a[0] : 256 * (a[0] + 1)])
-                else:
-                    nc.sync.dma_start(out=k1_raw[:], in_=k_hbm[:, :, 512:1024])
-            elif kind == "dm":
-                g = MCH[a[0]][a[1]]
-                nc.sync.dma_start(out=m_raw[a[0]][a[1]][:], in_=m_hbm[a[0]][:, :, P * g[0] : P * (g[-1] + 1)])
-            elif kind == "dv":
-                nc.sync.dma_start(out=v_raw[a[0]][:], in_=v[a[0]].rearrange("(c p j) e -> p c j e", p=P, j=4))
-            elif kind == "dt":
-                nc.sync.dma_start(out=t_sb[:, :, 0:4], in_=t.rearrange("(c p j) o -> p c (j o)", p=P, j=4))
-            elif kind == "ds":
-                with nc.allow_non_contiguous_dma(reason="one sink a query row"):
-                    nc.sync.dma_start(
-                        out=sink_sb[:].rearrange("p h a x -> p (h a) x")[:, :, 0:1],
-                        in_=sink.rearrange("h (a p) o -> p (h a) o", p=P),
-                    )
-            elif kind == "iq":
-                i, n = q_at[a[0]]
-                cnt = a[-1] - a[0] + 1
-                copy(
-                    eng,
-                    q_bf[:, P * a[0] : P * (a[-1] + 1), :].rearrange("p (a i) j -> p a j i", i=2),
-                    q_raw[i][:, :, P * n : P * (n + cnt)].rearrange("p j (a i) -> p a j i", i=2),
-                )
-            elif kind == "qq":
-                cols = slice(P * a[0], P * (a[-1] + 1))
-                quant(q_codes[:, cols], q_scales[:, cols], q_bf[:, cols, :].rearrange("p q j -> p (q j)"))
-            elif kind == "ik":
-                raw, bf = (k0_raw[a[0]], k0_bf[a[0]]) if a[0] < 2 else (k1_raw, k1_bf)
-                rs = slice(a[1], a[2] + 1)
-                copy(
-                    eng,
-                    bf[:, rs].rearrange("p r s j -> p s r j"),
-                    raw[:].rearrange("p j (s r) -> p s r j", r=4)[:, :, rs, :],
-                )
-            elif kind == "qk":
-                if a[0] < 2:
-                    cols = slice(64 * a[0], 64 * (a[0] + 1))
-                    for r in range(a[1], a[2] + 1):
-                        quant(k_codes[0][:, r, cols], k_scales[0][:, r, cols], k0_bf[a[0]][:, r].rearrange("p s j -> p (s j)"))
-                else:
-                    rs = slice(a[1], a[2] + 1)
-                    quant(
-                        k_codes[1][:, rs].rearrange("p r s -> p (r s)"),
-                        k_scales[1][:, rs].rearrange("p r s -> p (r s)"),
-                        k1_bf[:, rs].rearrange("p r s j -> p (r s j)"),
-                    )
-            elif kind == "iv":
-                h, c = a
-                copy(
-                    eng,
-                    v_bf[h][:, c].rearrange("p (a i) j -> p a j i", i=2),
-                    v_raw[h][:, c].rearrange("p j (a i) -> p a j i", i=2),
-                )
-            elif kind == "qv":
-                h = a[0]
-                quant(
-                    v_codes[h][:].rearrange("p c e -> p (c e)"),
-                    v_scales[h][:].rearrange("p c e -> p (c e)"),
-                    v_bf[h][:].rearrange("p c e j -> p (c e j)"),
-                )
-            elif kind == "mt":
-                c, i = a[0], a[1]
-                for j in range(a[2], a[3] + 1):
-                    if eng == "V":
-                        nc.vector.tensor_scalar(
-                            out=mt[c][i][:, j], in0=m_raw[c][i][:, j], scalar1=t_sb[:, c, j : j + 1], scalar2=None, op0=ALU.mult
-                        )
-                    else:
-                        nc.scalar.activation(out=mt[c][i][:, j], in_=m_raw[c][i][:, j], func=ACT.Copy, scale=t_sb[:, c, j : j + 1])
-            elif kind == "sc":
-                c, qt, h = a
-                rows = slice(64 * h, 64 * (h + 1))
-                cols = slice(P * qt, P * (qt + 1))
-                for r in range(4):
+        def quantise(codes, scales, src):
+            nc.vector.quantize_mx(out=codes.bitcast(FP8X4), scales=scales, in_=src)
+
+        def interleave(engine, dst, src):
+            cast(engine, dst.rearrange("p (a i) j -> p a j i", i=RUN), src.rearrange("p j (a i) -> p a j i", i=RUN))
+
+        def lay_queries(engine, qt):
+            n = 0 if qt in QUERY_LOADS[0] else 1
+            at = QUERY_LOADS[n].index(qt)
+            interleave(engine, q_bf[:, rows_of(qt, qt), :], q_raw[n][:, :, rows_of(at, at)])
+
+        def quantise_queries(qt):
+            cols = rows_of(qt, qt)
+            quantise(q_codes[:, cols], q_scales[:, cols], q_bf[:, cols, :].rearrange("p q j -> p (q j)"))
+
+        def lay_keys(engine, n, places):
+            share = slice(places.start, places.stop)
+            cast(
+                engine,
+                k_bf[n][:, share].rearrange("p r (a i) j -> p a j i r", i=RUN),
+                k_raw[n][:].rearrange("p j (a i r) -> p a j i r", i=RUN, r=PACK)[:, :, :, :, share],
+            )
+
+        def quantise_half_pass_keys(n, places):
+            cols = slice(KEY_LOADS[n][0] // PACK, KEY_LOADS[n][1] // PACK)
+            for r in places:
+                quantise(k_codes[0][:, r, cols], k_scales[0][:, r, cols], k_bf[n][:, r].rearrange("p s j -> p (s j)"))
+
+        def quantise_second_pass_keys(places):
+            share = slice(places.start, places.stop)
+            quantise(
+                k_codes[1][:, share].rearrange("p r s -> p (r s)"),
+                k_scales[1][:, share].rearrange("p r s -> p (r s)"),
+                k_bf[2][:, share].rearrange("p r s j -> p (r s j)"),
+            )
+
+        def lay_values(engine, h, c):
+            interleave(engine, v_bf[h][:, c], v_raw[h][:, c])
+
+        def quantise_values(h):
+            quantise(
+                v_codes[h][:].rearrange("p c e -> p (c e)"),
+                v_scales[h][:].rearrange("p c e -> p (c e)"),
+                v_bf[h][:].rearrange("p c e j -> p (c e j)"),
+            )
+
+        def scale_mask(engine, c, half, places):
+            for r in places:
+                times_column(engine, mask_t[c][half][:, r], mask_raw[c][half][:, r], t_cols[:, c, r : r + 1])
+
+        def scores(c, qt):
+            cols = rows_of(qt, qt)
+            for r in ALL_PLACES:
+                for h in BOTH_HEADS:
+                    rows = slice(HEAD_ROWS * h, HEAD_ROWS * (h + 1))
                     nc.tensor.matmul_mx(
-                        out=s_bank[h][qt % 2][:, r, :],
-                        lhsT=k_codes[c][rows, r, :].bitcast(X4),
+                        out=score_bank[h][qt % 2][:, r, :],
+                        lhsT=k_codes[c][rows, r, :].bitcast(FP8X4),
                         lhsT_scale=k_scales[c][rows, r, :],
-                        rhs=q_codes[rows, cols].bitcast(X4),
+                        rhs=q_codes[rows, cols].bitcast(FP8X4),
                         rhs_scale=q_scales[rows, cols],
                         start=True,
                         stop=True,
                     )
-            elif kind == "ex":
-                c, qt, h = a
-                nc.scalar.activation(
-                    out=pe[c][h][:, qt].rearrange("p (a r i) -> p a r i", r=4, i=2),
-                    in_=s_bank[h][qt % 2][:].rearrange("p r (a i) -> p a r i", i=2),
-                    func=ACT.Exp,
-                )
-            elif kind == "ww":
-                c, h, q0, q1 = a
-                i, n = m_at[c][q0]
-                cnt = q1 - q0 + 1
-                nc.vector.tensor_tensor(
-                    out=w_bf[c][h][:, P * q0 : P * (q1 + 1), :].rearrange("p (a i) r -> p a r i", i=2),
-                    in0=pe[c][h][:, q0 : q1 + 1].rearrange("p b (a r i) -> p (b a) r i", r=4, i=2),
-                    in1=mt[c][i][:, :, P * n : P * (n + cnt)].rearrange("p r (a i) -> p a r i", i=2),
-                    op=ALU.mult,
-                )
-            elif kind == "qw":
-                c, h, q0, q1 = a
-                cols = slice(P * q0, P * (q1 + 1))
-                quant(w_codes[c][h][:, cols], w_scales[c][h][:, cols], w_bf[c][h][:, cols, :].rearrange("p q j -> p (q j)"))
-            elif kind == "yy":
-                qt, h = a
-                cols = slice(P * qt, P * (qt + 1))
-                for c in range(2):
-                    nc.tensor.matmul_mx(
-                        out=y_bank[(2 * qt + h) % 4][:, 0:E],
-                        lhsT=w_codes[c][h][:, cols].bitcast(X4),
-                        lhsT_scale=w_scales[c][h][:, cols],
-                        rhs=v_codes[h][:, c, :].bitcast(X4),
-                        rhs_scale=v_scales[h][:, c, :],
-                        start=(c == 0),
-                        stop=(c == 1),
-                    )
-            elif kind == "de":
-                qt, h = a
-                y = y_bank[(2 * qt + h) % 4]
-                if eng == "V":
-                    nc.vector.tensor_scalar(
-                        out=den[:, qt, h : h + 1], in0=y[:, E - 1 : E], scalar1=sink_sb[:, h, qt, 0:1], scalar2=None, op0=ALU.add
-                    )
+
+        def exp(c, qt, h):
+            nc.scalar.activation(
+                out=exps[c][h][:, qt].rearrange("p (a r i) -> p a r i", r=PACK, i=RUN),
+                in_=score_bank[h][qt % 2][:].rearrange("p r (a i) -> p a r i", i=RUN),
+                func=ACT.Exp,
+            )
+
+        def weigh(c, h, first, last):
+            half, at = divmod(first, 2)
+            nc.vector.tensor_tensor(
+                out=w_bf[c][h][:, rows_of(first, last), :].rearrange("p (a i) r -> p a r i", i=RUN),
+                in0=exps[c][h][:, first : last + 1].rearrange("p b (a r i) -> p (b a) r i", r=PACK, i=RUN),
+                in1=mask_t[c][half][:, :, rows_of(at, at + last - first)].rearrange("p r (a i) -> p a r i", i=RUN),
+                op=ALU.mult,
+            )
+
+        def quantise_weights(c, h, first, last):
+            cols = rows_of(first, last)
+            quantise(w_codes[c][h][:, cols], w_scales[c][h][:, cols], w_bf[c][h][:, cols, :].rearrange("p q r -> p (q r)"))
+
+        def product(c, qt, h):
+            cols = rows_of(qt, qt)
+            nc.tensor.matmul_mx(
+                out=y_of(qt, h),
+                lhsT=w_codes[c][h][:, cols].bitcast(FP8X4),
+                lhsT_scale=w_scales[c][h][:, cols],
+                rhs=v_codes[h][:, c, :].bitcast(FP8X4),
+                rhs_scale=v_scales[h][:, c, :],
+                start=(c == 0),
+                stop=(c == PASSES - 1),
+            )
+
+        def add_sink(engine, qt, heads):
+            for h in heads:
+                dst, total = denom[:, qt, h : h + 1], y_of(qt, h)[:, VALUES - 1 : VALUES]
+                column = sink_cols[:, TILES * h + qt : TILES * h + qt + 1]
+                if engine == vector:
+                    nc.vector.tensor_scalar(out=dst, in0=total, scalar1=column, scalar2=None, op0=ALU.add)
                 else:
-                    nc.scalar.activation(out=den[:, qt, h : h + 1], in_=y[:, E - 1 : E], func=ACT.Identity, bias=sink_sb[:, h, qt, 0:1])
-            elif kind == "re":
-                qt, h0, h1 = a
-                nc.vector.reciprocal(out=rec[:, qt, h0 : h1 + 1], in_=den[:, qt, h0 : h1 + 1])
-            elif kind == "oo":
-                qt, h = a
-                y = y_bank[(2 * qt + h) % 4]
-                if eng == "V":
-                    nc.vector.tensor_scalar(
-                        out=res[qt][h][:], in0=y[:, 0:E], scalar1=rec[:, qt, h : h + 1], scalar2=None, op0=ALU.mult
-                    )
-                else:
-                    nc.scalar.activation(out=res[qt][h][:], in_=y[:, 0:E], func=ACT.Copy, scale=rec[:, qt, h : h + 1])
-                nc.sync.dma_start(out=out[h, P * qt : P * (qt + 1), :], in_=res[qt][h][:])
-            else:
-                raise ValueError(op)
+                    nc.scalar.activation(out=dst, in_=total, func=ACT.Identity, bias=column)
+
+        def invert(tiles, heads):
+            where = (slice(None), slice(tiles[0], tiles[-1] + 1), slice(heads[0], heads[-1] + 1))
+            nc.vector.reciprocal(out=inverse[where], in_=denom[where])
+
+        def finish(engine, qt, heads):
+            for h in heads:
+                times_column(engine, result[qt][:, h, :], y_of(qt, h), inverse[:, qt, h : h + 1])
+            these = slice(heads[0], heads[-1] + 1)
+            nc.sync.dma_start(out=out[these, rows_of(qt, qt), :].rearrange("h q e -> q h e"), in_=result[qt][:, these, :])
+
+        q_hbm = qT.rearrange("h (p j) q -> (h p) j q", j=PACK)
+        k_hbm = kT.rearrange("h (p j) n -> (h p) j n", j=PACK)
+        mask_hbm = mask.rearrange("(c s r) q -> c s r q", s=P, r=PACK)
+        sink_hbm = sink.rearrange("h (a b x) o -> b (h a) (x o)", b=P // BLOCK, x=BLOCK)
+
+        def load_keys(n):
+            nc.sync.dma_start(out=k_raw[n][:], in_=k_hbm[:, :, KEY_LOADS[n][0] : KEY_LOADS[n][1]])
+
+        def load_queries(n):
+            nc.sync.dma_start(out=q_raw[n][:], in_=q_hbm[:, :, rows_of(QUERY_LOADS[n][0], QUERY_LOADS[n][-1])])
+
+        def load_mask(c, half):
+            nc.sync.dma_start(out=mask_raw[c][half][:], in_=mask_hbm[c][:, :, HALF * half : HALF * (half + 1)])
+
+        def load_values(h):
+            nc.sync.dma_start(out=v_raw[h][:], in_=v[h].rearrange("(c s r) e -> s c r e", s=P, r=PACK))
 
         with tc.manual_schedule():
-            for op in ORDER.split():
-                run(op)
+            nc.gpsimd.memset(sink_rows[:], 0.0)
+            nc.scalar.activation(out=sink_rows[:], in_=sink_rows[:], func=ACT.Exp)
+
+            load_keys(0)
+            load_keys(1)
+            load_queries(0)
+            load_queries(1)
+            nc.sync.dma_start(out=t_cols[:, :, 0:PACK], in_=t.rearrange("(c s r) o -> s c (r o)", s=P, r=PACK))
+            load_mask(0, 0)
+            load_keys(2)
+            load_mask(0, 1)
+            load_mask(1, 0)
+            load_values(0)
+            load_values(1)
+            load_mask(1, 1)
+            for b in range(P // BLOCK):
+                nc.sync.dma_start(out=sink_rows[BLOCK * b : BLOCK * b + HEADS * TILES, :], in_=sink_hbm[b])
+
+            lay_keys(vector, 0, LOW)
+            lay_keys(vector, 0, HIGH)
+            quantise_half_pass_keys(0, LOW)
+            quantise_half_pass_keys(0, HIGH)
+            lay_keys(scalar, 1, LOW)
+            lay_keys(vector, 1, HIGH)
+            quantise_half_pass_keys(1, HIGH)
+            quantise_half_pass_keys(1, LOW)
+            lay_queries(scalar, 0)
+            quantise_queries(0)
+            scores(0, 0)
+            lay_queries(scalar, 2)
+            lay_queries(vector, 1)
+            lay_queries(vector, 3)
+            quantise_queries(1)
+            quantise_queries(2)
+            scores(0, 1)
+
+            exp(0, 0, 0)
+            exp(0, 0, 1)
+            scores(0, 2)
+            scale_mask(vector, 0, 0, ALL_PLACES)
+            quantise_queries(3)
+            exp(0, 1, 0)
+            exp(0, 1, 1)
+            scores(0, 3)
+            for qt in (0, 1):
+                for h in BOTH_HEADS:
+                    weigh(0, h, qt, qt)
+
+            exp(0, 2, 0)
+            lay_keys(scalar, 2, LOW)
+            lay_keys(vector, 2, HIGH)
+            quantise_second_pass_keys(LOW)
+            exp(0, 2, 1)
+            exp(0, 3, 0)
+            scale_mask(vector, 0, 1, LOW)
+            scale_mask(scalar, 0, 1, HIGH)
+            quantise_second_pass_keys(HIGH)
+            scores(1, 0)
+            quantise_weights(0, 0, 0, 1)
+            quantise_weights(0, 1, 0, 1)
+            exp(0, 3, 1)
+            scores(1, 1)
+            weigh(0, 0, 2, 3)
+            scale_mask(scalar, 1, 0, ALL_PLACES)
+            lay_values(vector, 0, 0)
+            lay_values(vector, 0, 1)
+            quantise_weights(0, 0, 2, 3)
+            quantise_values(0)
+            weigh(0, 1, 2, 3)
+
+            exp(1, 0, 0)
+            exp(1, 1, 0)
+            exp(1, 0, 1)
+            scores(1, 2)
+            lay_values(scalar, 1, 0)
+            exp(1, 1, 1)
+            scores(1, 3)
+            weigh(1, 0, 0, 1)
+            nc.vector.transpose(out=sink_cols[:], in_=sink_rows[:])
+            lay_values(scalar, 1, 1)
+            weigh(1, 1, 0, 1)
+            quantise_values(1)
+            quantise_weights(1, 0, 0, 1)
+            quantise_weights(0, 1, 2, 3)
+            quantise_weights(1, 1, 0, 1)
+            scale_mask(scalar, 1, 1, ALL_PLACES)
+            for qt in range(TILES):
+                product(0, qt, 0)
+            for c, h in ((1, 0), (0, 1), (1, 1)):
+                for qt in (0, 1):
+                    product(c, qt, h)
+
+            exp(1, 2, 0)
+            exp(1, 2, 1)
+            exp(1, 3, 0)
+            add_sink(scalar, 0, BOTH_HEADS)
+            add_sink(scalar, 1, BOTH_HEADS)
+            exp(1, 3, 1)
+            for h in BOTH_HEADS:
+                weigh(1, h, 2, 2)
+            for h in BOTH_HEADS:
+                quantise_weights(1, h, 2, 2)
+            invert((0, 1), BOTH_HEADS)
+            product(1, 2, 0)
+            product(0, 2, 1)
+            product(1, 2, 1)
+            finish(scalar, 0, BOTH_HEADS)
+            add_sink(scalar, 2, BOTH_HEADS)
+            finish(scalar, 1, BOTH_HEADS)
+
+            product(0, LAST_TILE, 1)
+            for h in BOTH_HEADS:
+                weigh(1, h, LAST_TILE, LAST_TILE)
+            quantise_weights(1, 0, LAST_TILE, LAST_TILE)
+            invert((2,), BOTH_HEADS)
+            quantise_weights(1, 1, LAST_TILE, LAST_TILE)
+            for h in BOTH_HEADS:
+                product(1, LAST_TILE, h)
+            finish(vector, 2, BOTH_HEADS)
+            add_sink(vector, LAST_TILE, BOTH_HEADS)
+            for h in BOTH_HEADS:
+                invert((LAST_TILE,), (h,))
+            finish(vector, LAST_TILE, (0,))
+            finish(scalar, LAST_TILE, (1,))

from contextlib import ExitStack

import concourse.mybir as mybir

HEADS, FEATURES, QUERIES, TOKENS, VALUES = 2, 256, 512, 1024, 128
FLOPS = 2 * HEADS * TOKENS * QUERIES * (FEATURES + VALUES)

F32 = mybir.dt.float32
BF16 = mybir.dt.bfloat16
U32 = mybir.dt.uint32
U8 = mybir.dt.uint8
FP8X4 = mybir.dt.float8_e4m3fn_x4
ACT = mybir.ActivationFunctionType
ALU = mybir.AluOpType

P = 128
PACK = 4
HEAD_ROWS = FEATURES // PACK
PASS = P * PACK
PASSES = TOKENS // PASS
TILES = QUERIES // P
HALF = QUERIES // 2
BLOCK = 32
RUN = 2

KEY_LOADS = ((0, PASS // 2), (PASS // 2, PASS), (PASS, 2 * PASS))
QUERY_LOADS = ((0,), (1, 2, 3))
LOW, HIGH, ALL_PLACES = range(0, 2), range(2, 4), range(0, 4)
BOTH_HEADS = (0, 1)
LAST_TILE = TILES - 1


def tile_rows_sink_mask_kernel(tc, qT, kT, t, v, mask, sink, out):
    nc = tc.nc
    vector, scalar = "vector", "scalar"

    with ExitStack() as ctx:
        sbuf = ctx.enter_context(tc.tile_pool(name="sbuf", bufs=1))
        psum = ctx.enter_context(tc.psum_pool(name="psum", bufs=1))

        def tile(name, shape, dtype):
            return sbuf.tile(shape, dtype, name=name, align_bytes=64)

        q_raw = [tile("q_raw%d" % n, [P, PACK, P * len(tiles)], F32) for n, tiles in enumerate(QUERY_LOADS)]
        q_bf = tile("q_bf", [P, QUERIES, PACK], BF16)
        q_codes = tile("q_codes", [P, QUERIES], U32)
        q_scales = tile("q_scales", [P, QUERIES], U8)
        k_raw = [tile("k_raw%d" % n, [P, PACK, hi - lo], F32) for n, (lo, hi) in enumerate(KEY_LOADS)]
        k_bf = [tile("k_bf%d" % n, [P, PACK, (hi - lo) // PACK, PACK], BF16) for n, (lo, hi) in enumerate(KEY_LOADS)]
        k_codes = [tile("k_codes%d" % c, [P, PACK, P], U32) for c in range(PASSES)]
        k_scales = [tile("k_scales%d" % c, [P, PACK, P], U8) for c in range(PASSES)]
        mask_raw = [[tile("mask_raw%d_%d" % (c, n), [P, PACK, HALF], F32) for n in range(2)] for c in range(PASSES)]
        mask_t = [[tile("mask_t%d_%d" % (c, n), [P, PACK, HALF], F32) for n in range(2)] for c in range(PASSES)]
        t_cols = tile("t_cols", [P, PASSES, 2 * PACK], F32)
        sink_rows = tile("sink_rows", [P, BLOCK], F32)
        sink_cols = tile("sink_cols", [P, BLOCK], F32)
        v_raw = [tile("v_raw%d" % h, [P, PASSES, PACK, VALUES], F32) for h in BOTH_HEADS]
        v_bf = [tile("v_bf%d" % h, [P, PASSES, VALUES, PACK], BF16) for h in BOTH_HEADS]
        v_codes = [tile("v_codes%d" % h, [P, PASSES, VALUES], U32) for h in BOTH_HEADS]
        v_scales = [tile("v_scales%d" % h, [P, PASSES, VALUES], U8) for h in BOTH_HEADS]
        exps = [[tile("exps%d_%d" % (c, h), [P, TILES, PACK * P], F32) for h in BOTH_HEADS] for c in range(PASSES)]
        w_bf = [[tile("w_bf%d_%d" % (c, h), [P, QUERIES, PACK], BF16) for h in BOTH_HEADS] for c in range(PASSES)]
        w_codes = [[tile("w_codes%d_%d" % (c, h), [P, QUERIES], U32) for h in BOTH_HEADS] for c in range(PASSES)]
        w_scales = [[tile("w_scales%d_%d" % (c, h), [P, QUERIES], U8) for h in BOTH_HEADS] for c in range(PASSES)]
        denom = tile("denom", [P, TILES, HEADS], F32)
        inverse = tile("inverse", [P, TILES, HEADS], F32)
        result = [tile("result%d" % qt, [P, HEADS, VALUES], F32) for qt in range(TILES)]

        score_bank = [[psum.tile([P, PACK, P], F32, name="score_bank%d_%d" % (h, b)) for b in range(2)] for h in BOTH_HEADS]
        y_bank = [psum.tile([P, PACK * P], F32, name="y_bank%d" % b) for b in range(TILES)]

        def y_of(qt, h):
            if (qt, h) == (LAST_TILE, 1):
                return y_bank[0][:, 0:VALUES]
            return y_bank[qt][:, VALUES * h : VALUES * (h + 1)]

        def rows_of(first, last):
            return slice(P * first, P * (last + 1))

        def cast(engine, dst, src):
            if engine == vector:
                nc.vector.tensor_copy(out=dst, in_=src)
            else:
                nc.scalar.copy(out=dst, in_=src)

        def times_column(engine, dst, src, column):
            if engine == vector:
                nc.vector.tensor_scalar(out=dst, in0=src, scalar1=column, scalar2=None, op0=ALU.mult)
            else:
                nc.scalar.activation(out=dst, in_=src, func=ACT.Copy, scale=column)

        def quantise(codes, scales, src):
            nc.vector.quantize_mx(out=codes.bitcast(FP8X4), scales=scales, in_=src)

        def interleave(engine, dst, src):
            cast(engine, dst.rearrange("p (a i) j -> p a j i", i=RUN), src.rearrange("p j (a i) -> p a j i", i=RUN))

        def lay_queries(engine, qt):
            n = 0 if qt in QUERY_LOADS[0] else 1
            at = QUERY_LOADS[n].index(qt)
            interleave(engine, q_bf[:, rows_of(qt, qt), :], q_raw[n][:, :, rows_of(at, at)])

        def quantise_queries(qt):
            cols = rows_of(qt, qt)
            quantise(q_codes[:, cols], q_scales[:, cols], q_bf[:, cols, :].rearrange("p q j -> p (q j)"))

        def lay_keys(engine, n, places):
            share = slice(places.start, places.stop)
            cast(
                engine,
                k_bf[n][:, share].rearrange("p r (a i) j -> p a j i r", i=RUN),
                k_raw[n][:].rearrange("p j (a i r) -> p a j i r", i=RUN, r=PACK)[:, :, :, :, share],
            )

        def quantise_half_pass_keys(n, places):
            cols = slice(KEY_LOADS[n][0] // PACK, KEY_LOADS[n][1] // PACK)
            for r in places:
                quantise(k_codes[0][:, r, cols], k_scales[0][:, r, cols], k_bf[n][:, r].rearrange("p s j -> p (s j)"))

        def quantise_second_pass_keys(places):
            share = slice(places.start, places.stop)
            quantise(
                k_codes[1][:, share].rearrange("p r s -> p (r s)"),
                k_scales[1][:, share].rearrange("p r s -> p (r s)"),
                k_bf[2][:, share].rearrange("p r s j -> p (r s j)"),
            )

        def lay_values(engine, h, c):
            interleave(engine, v_bf[h][:, c], v_raw[h][:, c])

        def quantise_values(h):
            quantise(
                v_codes[h][:].rearrange("p c e -> p (c e)"),
                v_scales[h][:].rearrange("p c e -> p (c e)"),
                v_bf[h][:].rearrange("p c e j -> p (c e j)"),
            )

        def scale_mask(engine, c, half, places):
            for r in places:
                times_column(engine, mask_t[c][half][:, r], mask_raw[c][half][:, r], t_cols[:, c, r : r + 1])

        def scores(c, qt):
            cols = rows_of(qt, qt)
            for r in ALL_PLACES:
                for h in BOTH_HEADS:
                    rows = slice(HEAD_ROWS * h, HEAD_ROWS * (h + 1))
                    nc.tensor.matmul_mx(
                        out=score_bank[h][qt % 2][:, r, :],
                        lhsT=k_codes[c][rows, r, :].bitcast(FP8X4),
                        lhsT_scale=k_scales[c][rows, r, :],
                        rhs=q_codes[rows, cols].bitcast(FP8X4),
                        rhs_scale=q_scales[rows, cols],
                        start=True,
                        stop=True,
                    )

        def exp(c, qt, h):
            nc.scalar.activation(
                out=exps[c][h][:, qt].rearrange("p (a r i) -> p a r i", r=PACK, i=RUN),
                in_=score_bank[h][qt % 2][:].rearrange("p r (a i) -> p a r i", i=RUN),
                func=ACT.Exp,
            )

        def weigh(c, h, first, last):
            half, at = divmod(first, 2)
            nc.vector.tensor_tensor(
                out=w_bf[c][h][:, rows_of(first, last), :].rearrange("p (a i) r -> p a r i", i=RUN),
                in0=exps[c][h][:, first : last + 1].rearrange("p b (a r i) -> p (b a) r i", r=PACK, i=RUN),
                in1=mask_t[c][half][:, :, rows_of(at, at + last - first)].rearrange("p r (a i) -> p a r i", i=RUN),
                op=ALU.mult,
            )

        def quantise_weights(c, h, first, last):
            cols = rows_of(first, last)
            quantise(w_codes[c][h][:, cols], w_scales[c][h][:, cols], w_bf[c][h][:, cols, :].rearrange("p q r -> p (q r)"))

        def product(c, qt, h):
            cols = rows_of(qt, qt)
            nc.tensor.matmul_mx(
                out=y_of(qt, h),
                lhsT=w_codes[c][h][:, cols].bitcast(FP8X4),
                lhsT_scale=w_scales[c][h][:, cols],
                rhs=v_codes[h][:, c, :].bitcast(FP8X4),
                rhs_scale=v_scales[h][:, c, :],
                start=(c == 0),
                stop=(c == PASSES - 1),
            )

        def add_sink(engine, qt, heads):
            for h in heads:
                dst, total = denom[:, qt, h : h + 1], y_of(qt, h)[:, VALUES - 1 : VALUES]
                column = sink_cols[:, TILES * h + qt : TILES * h + qt + 1]
                if engine == vector:
                    nc.vector.tensor_scalar(out=dst, in0=total, scalar1=column, scalar2=None, op0=ALU.add)
                else:
                    nc.scalar.activation(out=dst, in_=total, func=ACT.Identity, bias=column)

        def invert(tiles, heads):
            where = (slice(None), slice(tiles[0], tiles[-1] + 1), slice(heads[0], heads[-1] + 1))
            nc.vector.reciprocal(out=inverse[where], in_=denom[where])

        def finish(engine, qt, heads):
            for h in heads:
                times_column(engine, result[qt][:, h, :], y_of(qt, h), inverse[:, qt, h : h + 1])
            these = slice(heads[0], heads[-1] + 1)
            nc.sync.dma_start(out=out[these, rows_of(qt, qt), :].rearrange("h q e -> q h e"), in_=result[qt][:, these, :])

        q_hbm = qT.rearrange("h (p j) q -> (h p) j q", j=PACK)
        k_hbm = kT.rearrange("h (p j) n -> (h p) j n", j=PACK)
        mask_hbm = mask.rearrange("(c s r) q -> c s r q", s=P, r=PACK)
        sink_hbm = sink.rearrange("h (a b x) o -> b (h a) (x o)", b=P // BLOCK, x=BLOCK)

        def load_keys(n):
            nc.sync.dma_start(out=k_raw[n][:], in_=k_hbm[:, :, KEY_LOADS[n][0] : KEY_LOADS[n][1]])

        def load_queries(n):
            nc.sync.dma_start(out=q_raw[n][:], in_=q_hbm[:, :, rows_of(QUERY_LOADS[n][0], QUERY_LOADS[n][-1])])

        def load_mask(c, half):
            nc.sync.dma_start(out=mask_raw[c][half][:], in_=mask_hbm[c][:, :, HALF * half : HALF * (half + 1)])

        def load_values(h):
            nc.sync.dma_start(out=v_raw[h][:], in_=v[h].rearrange("(c s r) e -> s c r e", s=P, r=PACK))

        with tc.manual_schedule():
            nc.gpsimd.memset(sink_rows[:], 0.0)
            nc.scalar.activation(out=sink_rows[:], in_=sink_rows[:], func=ACT.Exp)

            load_keys(0)
            load_keys(1)
            load_queries(0)
            load_queries(1)
            nc.sync.dma_start(out=t_cols[:, :, 0:PACK], in_=t.rearrange("(c s r) o -> s c (r o)", s=P, r=PACK))
            load_mask(0, 0)
            load_keys(2)
            load_mask(0, 1)
            load_mask(1, 0)
            load_values(0)
            load_values(1)
            load_mask(1, 1)
            for b in range(P // BLOCK):
                nc.sync.dma_start(out=sink_rows[BLOCK * b : BLOCK * b + HEADS * TILES, :], in_=sink_hbm[b])

            lay_keys(vector, 0, LOW)
            lay_keys(vector, 0, HIGH)
            quantise_half_pass_keys(0, LOW)
            quantise_half_pass_keys(0, HIGH)
            lay_keys(scalar, 1, LOW)
            lay_keys(vector, 1, HIGH)
            quantise_half_pass_keys(1, HIGH)
            quantise_half_pass_keys(1, LOW)
            lay_queries(scalar, 0)
            quantise_queries(0)
            scores(0, 0)
            lay_queries(scalar, 2)
            lay_queries(vector, 1)
            lay_queries(vector, 3)
            quantise_queries(1)
            quantise_queries(2)
            scores(0, 1)

            exp(0, 0, 0)
            exp(0, 0, 1)
            scores(0, 2)
            scale_mask(vector, 0, 0, ALL_PLACES)
            quantise_queries(3)
            exp(0, 1, 0)
            exp(0, 1, 1)
            scores(0, 3)
            for qt in (0, 1):
                for h in BOTH_HEADS:
                    weigh(0, h, qt, qt)

            exp(0, 2, 0)
            lay_keys(scalar, 2, LOW)
            lay_keys(vector, 2, HIGH)
            quantise_second_pass_keys(LOW)
            exp(0, 2, 1)
            exp(0, 3, 0)
            scale_mask(vector, 0, 1, LOW)
            scale_mask(scalar, 0, 1, HIGH)
            quantise_second_pass_keys(HIGH)
            scores(1, 0)
            quantise_weights(0, 0, 0, 1)
            quantise_weights(0, 1, 0, 1)
            exp(0, 3, 1)
            scores(1, 1)
            weigh(0, 0, 2, 3)
            scale_mask(scalar, 1, 0, ALL_PLACES)
            lay_values(vector, 0, 0)
            lay_values(vector, 0, 1)
            quantise_weights(0, 0, 2, 3)
            quantise_values(0)
            weigh(0, 1, 2, 3)

            exp(1, 0, 0)
            exp(1, 1, 0)
            exp(1, 0, 1)
            scores(1, 2)
            lay_values(scalar, 1, 0)
            exp(1, 1, 1)
            scores(1, 3)
            weigh(1, 0, 0, 1)
            nc.vector.transpose(out=sink_cols[:], in_=sink_rows[:])
            lay_values(scalar, 1, 1)
            weigh(1, 1, 0, 1)
            quantise_values(1)
            quantise_weights(1, 0, 0, 1)
            quantise_weights(0, 1, 2, 3)
            quantise_weights(1, 1, 0, 1)
            scale_mask(scalar, 1, 1, ALL_PLACES)
            for qt in range(TILES):
                product(0, qt, 0)
            for c, h in ((1, 0), (0, 1), (1, 1)):
                for qt in (0, 1):
                    product(c, qt, h)

            exp(1, 2, 0)
            exp(1, 2, 1)
            exp(1, 3, 0)
            add_sink(scalar, 0, BOTH_HEADS)
            add_sink(scalar, 1, BOTH_HEADS)
            exp(1, 3, 1)
            for h in BOTH_HEADS:
                weigh(1, h, 2, 2)
            for h in BOTH_HEADS:
                quantise_weights(1, h, 2, 2)
            invert((0, 1), BOTH_HEADS)
            product(1, 2, 0)
            product(0, 2, 1)
            product(1, 2, 1)
            finish(scalar, 0, BOTH_HEADS)
            add_sink(scalar, 2, BOTH_HEADS)
            finish(scalar, 1, BOTH_HEADS)

            product(0, LAST_TILE, 1)
            for h in BOTH_HEADS:
                weigh(1, h, LAST_TILE, LAST_TILE)
            quantise_weights(1, 0, LAST_TILE, LAST_TILE)
            invert((2,), BOTH_HEADS)
            quantise_weights(1, 1, LAST_TILE, LAST_TILE)
            for h in BOTH_HEADS:
                product(1, LAST_TILE, h)
            finish(vector, 2, BOTH_HEADS)
            add_sink(vector, LAST_TILE, BOTH_HEADS)
            for h in BOTH_HEADS:
                invert((LAST_TILE,), (h,))
            finish(vector, LAST_TILE, (0,))
            finish(scalar, LAST_TILE, (1,))
